import numpy as np
import ml_dtypes


def mxq(x, axis, fmt="e4m3"):
    dtype, down = {"e4m3": (ml_dtypes.float8_e4m3fn, 7), "e5m2": (ml_dtypes.float8_e5m2, 14)}[fmt]
    v = np.moveaxis(np.asarray(x, np.float32).astype(ml_dtypes.bfloat16).astype(np.float64), axis, -1)
    blocks = v.reshape(v.shape[:-1] + (-1, 32))
    amax = np.abs(blocks).max(-1, keepdims=True)
    byte = np.maximum(np.where(amax > 0, np.frexp(amax)[1] - 1 + 127, 0) - down, 1)
    scale = np.exp2(byte - 127.0)
    codes = (blocks / scale).astype(np.float32).astype(dtype).astype(np.float64)
    return np.moveaxis((codes * scale).reshape(v.shape), -1, axis)


WIDE = False


def mx_kscale(k):
    if not WIDE:
        return np.ones(k)
    levels = np.array([10, -10, 5, -5, 0])
    if k % 512:
        return np.exp2(np.random.permutation(np.resize(levels, k // 32))).repeat(32)
    a = np.empty((k // 512, 16))
    for p in range(k // 512):
        a[p, :8] = np.random.permutation(np.resize(levels, 8))
        for g in range(8):
            far = levels[np.abs(levels - a[p, g]) >= 10]
            a[p, g + 8] = far[np.random.randint(len(far))]
    return np.exp2(a.ravel()).repeat(32)


def f64(x):
    return np.asarray(x).astype(np.float64)


def striped(idx):
    return np.tile(idx.reshape(-1, 16).T, (8, 1)).astype(np.uint16)


def unstriped(offs):
    return offs[:16].T.reshape(-1).astype(np.int64)


def pack_weight(w):
    k, n = w.shape
    w = f64(np.asarray(w, np.float32).astype(ml_dtypes.bfloat16)).reshape(k // 32, 32, n)
    amax = np.abs(w).max(1)
    byte = np.clip(np.where(amax > 0, np.frexp(amax)[1] - 1 + 127 - 7, 1), 1, 254)
    scaled = (w * np.exp2(127.0 - byte)[:, None, :]).reshape(k, n).astype(np.float32)
    words = np.ascontiguousarray(scaled.reshape(k // 512, 128, 4, n).transpose(0, 1, 3, 2)).astype(ml_dtypes.float8_e4m3fn).view(np.uint8)
    return words, np.ascontiguousarray(byte.astype(np.uint8).reshape(k // 512, 16, n))


def unpack_weight(words, scales):
    g, p, n, _ = words.shape
    vals = np.ascontiguousarray(words).view(ml_dtypes.float8_e4m3fn).astype(np.float64) * np.repeat(np.exp2(scales.astype(np.float64) - 127.0), 8, axis=1)[..., None]
    return vals.transpose(0, 1, 3, 2).reshape(g * 512, n)


E2M1 = np.array([0.0, 0.5, 1.0, 1.5, 2.0, 3.0, 4.0, 6.0, -0.0, -0.5, -1.0, -1.5, -2.0, -3.0, -4.0, -6.0])


def pack_fp4(w):
    k, n = w.shape
    w = f64(np.asarray(w, np.float32).astype(ml_dtypes.bfloat16)).reshape(k // 32, 32, n)
    amax = np.abs(w).max(1)
    mant, ex = np.frexp(amax / 6.0)
    byte = np.clip(np.where(amax > 0, np.where(mant > 0.5, ex, ex - 1) + 127, 1), 1, 254)
    scaled = (w * np.exp2(127.0 - byte)[:, None, :]).reshape(k, n).astype(np.float32)
    c = np.ascontiguousarray(scaled.reshape(k // 512, 128, 4, n).transpose(0, 1, 3, 2)).astype(ml_dtypes.float4_e2m1fn).view(np.uint8) & 0xF
    words = (c[..., 0::2] | (c[..., 1::2] << 4)).reshape(k // 512, 128, 2 * n)
    return np.ascontiguousarray(words), np.ascontiguousarray(byte.astype(np.uint8).reshape(k // 512, 16, n))


def unpack_fp4(words, scales):
    g, _, n = scales.shape
    words = np.ascontiguousarray(words).reshape(g, 128, n, 2)
    nib = np.empty((g, 128, n, 4), np.uint8)
    nib[..., 0::2] = words & 0xF
    nib[..., 1::2] = words >> 4
    vals = E2M1[nib] * np.repeat(np.exp2(scales.astype(np.float64) - 127.0), 8, axis=1)[..., None]
    return vals.transpose(0, 1, 3, 2).reshape(g * 512, n)


K, T, S, D, N, H, V, U = 512, 2048, 1024, 2, 256, 512, 512, 512


def setup_inputs():
    n = np.random.standard_normal
    s = mx_kscale(K)[:, None]
    u = mx_kscale(H)
    packed_xT = pack_weight(n((K, T)) * s)
    packed_w1 = pack_fp4(n((K, H)) / np.sqrt(K) / s)
    packed_w2 = pack_fp4(n((K, H)) / np.sqrt(K) / s)
    packed_w3 = pack_fp4(n((H, N)) / np.sqrt(H) / u[:, None])
    return {
        "x_words": packed_xT[0],
        "x_scales": packed_xT[1],
        "w1_words": packed_w1[0],
        "w1_scales": packed_w1[1],
        "w2_words": packed_w2[0],
        "w2_scales": packed_w2[1],
        "unit": (np.random.uniform(0.6, 1.4, (H, 1)) * u[:, None]).astype(np.float32),
        "w3_words": packed_w3[0],
        "w3_scales": packed_w3[1],
        "offs": striped(np.random.permutation(T)[:S]),
        "s1": striped(np.random.randint(0, V, U)),
        "s2": striped(np.random.randint(0, V, U)),
    }


def reference(x_words, x_scales, w1_words, w1_scales, w2_words, w2_scales, unit, w3_words, w3_scales, offs, s1, s2):
    xq = unpack_weight(x_words, x_scales)[:, unstriped(offs)]
    re = unpack_fp4(w1_words, w1_scales).T @ xq
    im2 = unpack_fp4(w2_words, w2_scales).T @ xq
    pw = (re) ** 2 + (im2) ** 2
    p11 = pw.reshape(len(pw), -1, D).sum(axis=2) + 0.4
    pa1 = p11[:, unstriped(s1)]
    cx = re * (np.pad(re, ((0, 0), (0, 1)))[:, 1:]) + im2 * (np.pad(im2, ((0, 0), (0, 1)))[:, 1:])
    p12 = cx.reshape(len(cx), -1, D).sum(axis=2)
    pd1 = p12[:, unstriped(s1)]
    pa2 = p11[:, unstriped(s2)]
    spec = (pa1 - pd1) / (pa2 + 0.5)
    pd2 = p12[:, unstriped(s2)]
    hid = f64(unit) * (spec * np.tanh(pd2))
    return unpack_fp4(w3_words, w3_scales).T @ mxq(hid, 0, "e4m3")

@@ -1,0 +1,267 @@
+from contextlib import ExitStack
+
+import concourse.mybir as mybir
+
+K, T, S, H, V, N = 512, 2048, 1024, 512, 512, 256
+FLOPS = 2 * K * H * S * 2 + 2 * H * N * V
+
+F32 = mybir.dt.float32
+BF16 = mybir.dt.bfloat16
+I32 = mybir.dt.int32
+U32 = mybir.dt.uint32
+U16 = mybir.dt.uint16
+U8 = mybir.dt.uint8
+FP8X4 = mybir.dt.float8_e4m3fn_x4
+FP4X4 = mybir.dt.float4_e2m1fn_x4
+ACT = mybir.ActivationFunctionType
+ALU = mybir.AluOpType
+
+P = 128
+PACK = 4
+BANK = 512
+HALF = 256
+
+
+def tile_picked_ybeamfr_mul_p_kernel(
+    tc, x_words, x_scales, w1_words, w1_scales, w2_words, w2_scales, unit, w3_words, w3_scales, offs, s1, s2, out
+):
+    nc = tc.nc
+    with ExitStack() as ctx:
+        keep = ctx.enter_context(tc.tile_pool(name="keep", bufs=1))
+        ring = ctx.enter_context(tc.tile_pool(name="ring", bufs=2))
+        psum = ctx.enter_context(tc.psum_pool(name="psum", bufs=8))
+
+        offs_t = keep.tile([P, S // 16], U16, name="offs_t")
+        s1_t = keep.tile([P, V // 16], U16, name="s1_t")
+        s2_t = keep.tile([P, V // 16], U16, name="s2_t")
+        xw_raw = keep.tile([P, T], I32, name="xw_raw", align_bytes=64)
+        xs_raw = keep.tile([P, T], U8, name="xs_raw", align_bytes=64)
+        ww_raw = keep.tile([P, 2, 2 * H], U8, name="ww_raw", align_bytes=64)
+        ws_raw = keep.tile([P, 2, H], U8, name="ws_raw", align_bytes=64)
+        w3w = keep.tile([P, 2 * N], U8, name="w3w", align_bytes=64)
+        w3s = keep.tile([P, N], U8, name="w3s", align_bytes=64)
+        unit_t = keep.tile([P, PACK], F32, name="unit_t")
+        evens = keep.tile([P, PACK, 2, V + 8], F32, name="evens")
+
+        nc.vector.memset(xs_raw[:].bitcast(I32), 0)
+        nc.gpsimd.memset(ws_raw[:].bitcast(I32), 0)
+
+        def load_scales(queue, plane, rows, q):
+            queue.dma_start(out=plane[32 * q : 32 * q + 4].bitcast(I32), in_=rows[0, 4 * q : 4 * q + 4, :].bitcast(I32))
+
+        nc.sync.dma_start(offs_t[:], offs)
+        nc.scalar.dma_start(out=ww_raw[:, 0].bitcast(I32), in_=w1_words[0].bitcast(I32))
+        for q in range(4):
+            load_scales(nc.scalar if q % 2 else nc.sync, xs_raw[:], x_scales, q)
+        nc.scalar.dma_start(out=xw_raw[:], in_=x_words[0].rearrange("p c r -> p (c r)").bitcast(I32))
+        for q in range(4):
+            load_scales(nc.sync, ws_raw[:, 0], w1_scales, q)
+        nc.sync.dma_start(out=ww_raw[:, 1].bitcast(I32), in_=w2_words[0].bitcast(I32))
+        for q in range(4):
+            load_scales(nc.sync, ws_raw[:, 1], w2_scales, q)
+        nc.gpsimd.memset(evens[:, :, :, V : V + 1], 0.0)
+        nc.gpsimd.memset(w3s[:].bitcast(I32), 0)
+        nc.sync.dma_start(s1_t[:], s1)
+        nc.sync.dma_start(s2_t[:], s2)
+        nc.gpsimd.dma_start(out=unit_t[:], in_=unit.rearrange("(p t) o -> p (t o)", t=PACK))
+        nc.gpsimd.dma_start(out=w3w[:].bitcast(I32), in_=w3_words[0].bitcast(I32))
+        for q in range(4):
+            load_scales(nc.sync, w3s[:], w3_scales, q)
+
+        xw = [keep.tile([P, BANK], U32, name=f"xw{h}", align_bytes=64) for h in range(2)]
+        xs = [keep.tile([P, BANK], U8, name=f"xs{h}", align_bytes=64) for h in range(2)]
+        ww_first = [keep.tile([P, 2 * P], U8, name=f"ww_first{w}", align_bytes=64) for w in range(2)]
+        ws_first = [keep.tile([P, P], U8, name=f"ws_first{w}", align_bytes=64) for w in range(2)]
+        ww_rest = keep.tile([P, 2, PACK - 1, 2 * P], U8, name="ww_rest", align_bytes=64)
+        ws_rest = keep.tile([P, 2, PACK - 1, P], U8, name="ws_rest", align_bytes=64)
+        words_by_t = ww_raw[:].rearrange("p w (m t b) -> p w t m b", t=PACK, b=2)
+        scales_by_t = ws_raw[:].rearrange("p w (m t) -> p w t m", t=PACK)
+
+        def gather_scales(h):
+            nc.vector.tensor_copy(xs[h][:], xs_raw[:].indirect(offs_t[:, 32 * h : 32 * (h + 1)]))
+
+        def gather_words(h):
+            nc.vector.tensor_copy(xw[h][:], xw_raw[:].bitcast(U32).indirect(offs_t[:, 32 * h : 32 * (h + 1)]))
+
+        def deal_first(w):
+            nc.vector.tensor_copy(out=ww_first[w][:].rearrange("p (m b) -> p m b", b=2), in_=words_by_t[:, w, 0])
+            nc.vector.tensor_copy(out=ws_first[w][:], in_=scales_by_t[:, w, 0])
+
+        gather_scales(0)
+        gather_words(0)
+        deal_first(0)
+        deal_first(1)
+        gather_scales(1)
+        gather_words(1)
+        nc.vector.tensor_copy(out=ww_rest[:].rearrange("p w t (m b) -> p w t m b", b=2), in_=words_by_t[:, :, 1:])
+        nc.vector.tensor_copy(out=ws_rest[:], in_=scales_by_t[:, :, 1:])
+
+        noise = [keep.tile([P, 2 * V], F32, name=f"noise{t}") for t in range(PACK)]
+        logd = [keep.tile([P, V], F32, name=f"logd{t}") for t in range(PACK - 1)]
+        logd.append(keep.tile([P, V], F32, name="logd_last", tag="hold"))
+        noise_g = [keep.tile([P, V], F32, name=f"noise_g{t}") for t in range(PACK)]
+        power = [keep.tile([P, V], F32, name=f"power{t}") for t in range(PACK)]
+
+        def products(t):
+            banks = {}
+            for h in range(2):
+                for w in range(2):
+                    bank = psum.tile([P, BANK], F32, name="bank")
+                    nc.tensor.matmul_mx(
+                        out=bank[:],
+                        lhsT=(ww_rest[:, w, t - 1] if t else ww_first[w][:]).bitcast(FP4X4),
+                        lhsT_scale=ws_rest[:, w, t - 1] if t else ws_first[w][:],
+                        rhs=xw[h][:].bitcast(FP8X4),
+                        rhs_scale=xs[h][:],
+                        start=True,
+                        stop=True,
+                    )
+                    banks[w, h] = bank[:].rearrange("p (v e) -> p e v", e=2)
+            return banks
+
+        def copy_evens(t, banks):
+            for h in range(2):
+                for w in range(2):
+                    nc.scalar.copy(out=evens[:, t, w, HALF * h : HALF * (h + 1)], in_=banks[w, h][:, 0, :])
+
+        def squares(banks):
+            sq = ring.tile([P, 2, 2, V], F32, name="sq")
+            for h in range(2):
+                for w in range(2):
+                    nc.scalar.activation(out=sq[:, w, :, HALF * h : HALF * (h + 1)], in_=banks[w, h], func=ACT.Square)
+            return sq
+
+        def add_parts(sq):
+            pw = ring.tile([P, 2, V], F32, name="pw")
+            nc.vector.tensor_tensor(pw[:], sq[:, 0], sq[:, 1], ALU.add)
+            return pw
+
+        def add_pairs(t, pw):
+            nc.vector.tensor_tensor(power[t][:], pw[:, 0], pw[:, 1], ALU.add)
+
+        def neighbours(t):
+            nb = ring.tile([P, 2, V], F32, name="nb")
+            nc.vector.tensor_tensor(nb[:], evens[:, t, :, 0:V], evens[:, t, :, 1 : V + 1], ALU.add)
+            return nb
+
+        def cross(nb, banks):
+            cx = ring.tile([P, 2, V], F32, name="cx")
+            for h in range(2):
+                for w in range(2):
+                    cols = slice(HALF * h, HALF * (h + 1))
+                    nc.vector.tensor_tensor(cx[:, w, cols], banks[w, h][:, 1, :], nb[:, w, cols], ALU.mult)
+            return cx
+
+        def add_cross(t, cx):
+            nc.vector.tensor_tensor(noise[t][:, V:], cx[:, 0], cx[:, 1], ALU.add)
+
+        def make_noise(t):
+            nc.vector.scalar_tensor_tensor(noise[t][:, :V], power[t][:], 0.4, noise[t][:, V:], ALU.add, ALU.subtract)
+
+        def log_power(t):
+            nc.scalar.activation(out=logd[t][:], in_=power[t][:], func=ACT.Ln, bias=0.9)
+
+        def gather_noise(t):
+            nc.scalar.activation(out=noise_g[t][:], in_=noise[t][:].indirect(s1_t[:]), func=ACT.Copy)
+
+        last = PACK - 1
+        for t in range(last):
+            banks = products(t)
+            copy_evens(t, banks)
+            sq = squares(banks)
+            nb = neighbours(t)
+            if t > 0:
+                make_noise(t - 1)
+                log_power(t - 1)
+            cx = cross(nb, banks)
+            pw = add_parts(sq)
+            add_cross(t, cx)
+            add_pairs(t, pw)
+            if t > 0:
+                gather_noise(t - 1)
+        banks = products(last)
+        sq = squares(banks)
+        log_power(last - 1)
+        copy_evens(last, banks)
+        pw = add_parts(sq)
+        make_noise(last - 1)
+        add_pairs(last, pw)
+        log_power(last)
+        gather_noise(last - 1)
+        nb = neighbours(last)
+        cx = cross(nb, banks)
+        add_cross(last, cx)
+        make_noise(last)
+
+        inv_last = keep.tile([P, V], F32, name="inv_last")
+        nc.scalar.activation(out=inv_last[:], in_=logd[last][:], func=ACT.Exp, scale=-1.0)
+        late = keep.tile([P, 2 * PACK - 1, V], F32, name="late", tag="hold")
+        gain = [keep.tile([P, V], F32, name=f"gain{t}") for t in range(PACK)]
+        hid = keep.tile([P, PACK, V], F32, name="hid")
+
+        def finish(h):
+            cols = slice(HALF * h, HALF * (h + 1))
+            hb = keep.tile([P, HALF, PACK], BF16, name=f"hb{h}", align_bytes=64)
+            nc.vector.tensor_copy(
+                out=hb[:].rearrange("p (c i) t -> p c t i", i=4),
+                in_=hid[:, :, cols].rearrange("p t (c i) -> p c t i", i=4),
+            )
+            return hb
+
+        def last_product(h, hb):
+            cols = slice(HALF * h, HALF * (h + 1))
+            codes = keep.tile([P, HALF], U32, name=f"codes{h}", align_bytes=64)
+            scales = keep.tile([P, HALF], U8, name=f"scales{h}", align_bytes=64)
+            nc.vector.quantize_mx(out=codes[:].bitcast(FP8X4), scales=scales[:], in_=hb[:].rearrange("p c t -> p (c t)"))
+            bank = psum.tile([P, BANK], F32, name="bank")
+            for m in range(2):
+                nc.tensor.matmul_mx(
+                    out=bank[:, HALF * m : HALF * (m + 1)],
+                    lhsT=w3w[:, 2 * P * m : 2 * P * (m + 1)].bitcast(FP4X4),
+                    lhsT_scale=w3s[:, P * m : P * (m + 1)],
+                    rhs=codes[:].bitcast(FP8X4),
+                    rhs_scale=scales[:],
+                    start=True,
+                    stop=True,
+                )
+            res = keep.tile([P, 2, HALF], F32, name=f"res{h}")
+            nc.scalar.copy(out=res[:].rearrange("p m v -> p (m v)"), in_=bank[:])
+            nc.sync.dma_start(out=out[:, cols].rearrange("(m p) v -> p m v", p=P), in_=res[:])
+
+        def gather_gain(t, h):
+            cols = slice(HALF * h, HALF * (h + 1))
+            nc.vector.tensor_tensor(hid[:, t, cols], gain[t][:].indirect(s2_t[:, 16 * h : 16 * (h + 1)]), noise_g[t][:, cols], ALU.mult)
+
+        def gather_gain_scalar(t):
+            picked = ring.tile([P, V], F32, name="picked")
+            for h in range(2):
+                cols = slice(HALF * h, HALF * (h + 1))
+                nc.scalar.activation(out=picked[:, cols], in_=gain[t][:].indirect(s2_t[:, 16 * h : 16 * (h + 1)]), func=ACT.Copy)
+            return picked
+
+        def make_gain(t):
+            if t < last:
+                inv = late[:, PACK + t]
+                nc.scalar.activation(out=inv, in_=logd[t][:], func=ACT.Exp, scale=-1.0)
+            else:
+                inv = inv_last[:]
+            nc.scalar.activation(out=late[:, t], in_=noise[t][:, V:], func=ACT.Tanh)
+            nc.vector.scalar_tensor_tensor(gain[t][:], late[:, t], unit_t[:, t : t + 1], inv, ALU.mult, ALU.mult)
+
+        make_gain(0)
+        make_gain(1)
+        gather_gain(0, 0)
+        gather_gain(0, 1)
+        make_gain(2)
+        make_gain(3)
+        gather_noise(3)
+        picked = gather_gain_scalar(2)
+        gather_gain(1, 0)
+        gather_gain(1, 1)
+        gather_gain(3, 0)
+        nc.vector.tensor_tensor(hid[:, 2], picked[:], noise_g[2][:], ALU.mult)
+        hb0 = finish(0)
+        gather_gain(last, 1)
+        last_product(0, hb0)
+        hb1 = finish(1)
+        last_product(1, hb1)

@@ -1,6 +1,7 @@
 from contextlib import ExitStack
 
 import concourse.mybir as mybir
+from concourse.masks import make_identity
 
 K, T, S, H, V, N = 512, 2048, 1024, 512, 512, 256
 FLOPS = 2 * K * H * S * 2 + 2 * H * N * V
@@ -29,37 +30,42 @@ def tile_picked_ybeamfr_mul_p_kernel(
     with ExitStack() as ctx:
         keep = ctx.enter_context(tc.tile_pool(name="keep", bufs=1))
         ring = ctx.enter_context(tc.tile_pool(name="ring", bufs=2))
-        psum = ctx.enter_context(tc.psum_pool(name="psum", bufs=8))
+        quad = ctx.enter_context(tc.tile_pool(name="quad", bufs=4))
+        psum = ctx.enter_context(tc.psum_pool(name="psum", bufs=4))
 
         offs_t = keep.tile([P, S // 16], U16, name="offs_t")
         s1_t = keep.tile([P, V // 16], U16, name="s1_t")
         s2_t = keep.tile([P, V // 16], U16, name="s2_t")
         xw_raw = keep.tile([P, T], I32, name="xw_raw", align_bytes=64)
         xs_raw = keep.tile([P, T], U8, name="xs_raw", align_bytes=64)
-        ww_raw = keep.tile([P, 2, 2 * H], U8, name="ww_raw", align_bytes=64)
-        ws_raw = keep.tile([P, 2, H], U8, name="ws_raw", align_bytes=64)
+        ww = [keep.tile([P, 2 * H], U8, name=f"ww{w}", align_bytes=64) for w in range(2)]
+        ws = [keep.tile([P, H], U8, name=f"ws{w}", align_bytes=64) for w in range(2)]
         w3w = keep.tile([P, 2 * N], U8, name="w3w", align_bytes=64)
         w3s = keep.tile([P, N], U8, name="w3s", align_bytes=64)
         unit_t = keep.tile([P, PACK], F32, name="unit_t")
-        evens = keep.tile([P, PACK, 2, V + 8], F32, name="evens")
+        ident = keep.tile([P, P], F32, name="ident")
+        next_w = keep.tile([P, HALF], U32, name="next_w", align_bytes=64)
+        next_s = keep.tile([P, HALF], U8, name="next_s", align_bytes=64)
 
-        nc.vector.memset(xs_raw[:].bitcast(I32), 0)
-        nc.gpsimd.memset(ws_raw[:].bitcast(I32), 0)
+        nc.gpsimd.memset(xs_raw[:].bitcast(I32), 0)
+        nc.gpsimd.memset(ws[1][:].bitcast(I32), 0)
+        nc.gpsimd.memset(ws[0][:].bitcast(I32), 0)
 
         def load_scales(queue, plane, rows, q):
             queue.dma_start(out=plane[32 * q : 32 * q + 4].bitcast(I32), in_=rows[0, 4 * q : 4 * q + 4, :].bitcast(I32))
 
         nc.sync.dma_start(offs_t[:], offs)
-        nc.scalar.dma_start(out=ww_raw[:, 0].bitcast(I32), in_=w1_words[0].bitcast(I32))
+        nc.sync.dma_start(out=xw_raw[:], in_=x_words[0].rearrange("p c r -> p (c r)").bitcast(I32))
         for q in range(4):
-            load_scales(nc.scalar if q % 2 else nc.sync, xs_raw[:], x_scales, q)
-        nc.scalar.dma_start(out=xw_raw[:], in_=x_words[0].rearrange("p c r -> p (c r)").bitcast(I32))
+            load_scales(nc.scalar, xs_raw[:], x_scales, q)
+        nc.gpsimd.dma_start(out=ww[0][:].bitcast(I32), in_=w1_words[0].bitcast(I32))
+        nc.gpsimd.dma_start(out=ww[1][:].bitcast(I32), in_=w2_words[0].bitcast(I32))
         for q in range(4):
-            load_scales(nc.sync, ws_raw[:, 0], w1_scales, q)
-        nc.sync.dma_start(out=ww_raw[:, 1].bitcast(I32), in_=w2_words[0].bitcast(I32))
-        for q in range(4):
-            load_scales(nc.sync, ws_raw[:, 1], w2_scales, q)
-        nc.gpsimd.memset(evens[:, :, :, V : V + 1], 0.0)
+            load_scales(nc.scalar, ws[1][:], w2_scales, q)
+            load_scales(nc.sync, ws[0][:], w1_scales, q)
+        nc.vector.memset(next_w[:, HALF - 8 :].bitcast(I32), 0)
+        nc.vector.memset(next_s[:, HALF - 32 :].bitcast(I32), 0)
+        make_identity(nc, ident[:])
         nc.gpsimd.memset(w3s[:].bitcast(I32), 0)
         nc.sync.dma_start(s1_t[:], s1)
         nc.sync.dma_start(s2_t[:], s2)
@@ -68,155 +74,165 @@ def tile_picked_ybeamfr_mul_p_kernel(
         for q in range(4):
             load_scales(nc.sync, w3s[:], w3_scales, q)
 
-        xw = [keep.tile([P, BANK], U32, name=f"xw{h}", align_bytes=64) for h in range(2)]
-        xs = [keep.tile([P, BANK], U8, name=f"xs{h}", align_bytes=64) for h in range(2)]
-        ww_first = [keep.tile([P, 2 * P], U8, name=f"ww_first{w}", align_bytes=64) for w in range(2)]
-        ws_first = [keep.tile([P, P], U8, name=f"ws_first{w}", align_bytes=64) for w in range(2)]
-        ww_rest = keep.tile([P, 2, PACK - 1, 2 * P], U8, name="ww_rest", align_bytes=64)
-        ws_rest = keep.tile([P, 2, PACK - 1, P], U8, name="ws_rest", align_bytes=64)
-        words_by_t = ww_raw[:].rearrange("p w (m t b) -> p w t m b", t=PACK, b=2)
-        scales_by_t = ws_raw[:].rearrange("p w (m t) -> p w t m", t=PACK)
+        xw = [keep.tile([P, PACK, P], U32, name=f"xw{h}", align_bytes=64) for h in range(2)]
+        xs = [keep.tile([P, PACK, P], U8, name=f"xs{h}", align_bytes=64) for h in range(2)]
 
-        def gather_scales(h):
-            nc.vector.tensor_copy(xs[h][:], xs_raw[:].indirect(offs_t[:, 32 * h : 32 * (h + 1)]))
+        def pick(h, window, dealt, dtype, line, name, tag):
+            picked_x = keep.tile([P, BANK], dtype, name=name, tag=tag, align_bytes=64)
+            nc.vector.tensor_copy(picked_x[:], window.indirect(offs_t[:, 32 * h : 32 * (h + 1)]))
+            nc.vector.tensor_copy(
+                out=dealt[:].rearrange("p r (c i) -> p c r i", i=line),
+                in_=picked_x[:].rearrange("p (c i r) -> p c r i", i=line, r=PACK),
+            )
 
-        def gather_words(h):
-            nc.vector.tensor_copy(xw[h][:], xw_raw[:].bitcast(U32).indirect(offs_t[:, 32 * h : 32 * (h + 1)]))
+        def pick_half(h):
+            pick(h, xs_raw[:], xs[h], U8, 16, f"ps{h}", "picked" if h else "picked_first")
+            pick(h, xw_raw[:].bitcast(U32), xw[h], U32, 4, f"pw{h}", "picked")
 
-        def deal_first(w):
-            nc.vector.tensor_copy(out=ww_first[w][:].rearrange("p (m b) -> p m b", b=2), in_=words_by_t[:, w, 0])
-            nc.vector.tensor_copy(out=ws_first[w][:], in_=scales_by_t[:, w, 0])
+        def shift():
+            for shifted, dealt in ((next_w, xw), (next_s, xs)):
+                nc.vector.tensor_copy(out=shifted[:, 0 : P - 1], in_=dealt[0][:, 0, 1:])
+                nc.vector.tensor_copy(out=shifted[:, P - 1 : 2 * P - 1], in_=dealt[1][:, 0, :])
 
-        gather_scales(0)
-        gather_words(0)
-        deal_first(0)
-        deal_first(1)
-        gather_scales(1)
-        gather_words(1)
-        nc.vector.tensor_copy(out=ww_rest[:].rearrange("p w t (m b) -> p w t m b", b=2), in_=words_by_t[:, :, 1:])
-        nc.vector.tensor_copy(out=ws_rest[:], in_=scales_by_t[:, :, 1:])
-
-        noise = [keep.tile([P, 2 * V], F32, name=f"noise{t}") for t in range(PACK)]
-        logd = [keep.tile([P, V], F32, name=f"logd{t}") for t in range(PACK - 1)]
-        logd.append(keep.tile([P, V], F32, name="logd_last", tag="hold"))
+        noise = [keep.tile([P, V], F32, name=f"noise{t}") for t in range(PACK)]
+        corr = keep.tile([P, PACK, V], F32, name="corr")
+        logd = [keep.tile([P, 2, V], F32, name="logd0"), keep.tile([P, 2, V], F32, name="logd1", tag="hold")]
         noise_g = [keep.tile([P, V], F32, name=f"noise_g{t}") for t in range(PACK)]
-        power = [keep.tile([P, V], F32, name=f"power{t}") for t in range(PACK)]
 
-        def products(t):
+        def products(h, order):
             banks = {}
-            for h in range(2):
-                for w in range(2):
-                    bank = psum.tile([P, BANK], F32, name="bank")
-                    nc.tensor.matmul_mx(
-                        out=bank[:],
-                        lhsT=(ww_rest[:, w, t - 1] if t else ww_first[w][:]).bitcast(FP4X4),
-                        lhsT_scale=ws_rest[:, w, t - 1] if t else ws_first[w][:],
-                        rhs=xw[h][:].bitcast(FP8X4),
-                        rhs_scale=xs[h][:],
-                        start=True,
-                        stop=True,
-                    )
-                    banks[w, h] = bank[:].rearrange("p (v e) -> p e v", e=2)
+            for w, r in order:
+                cols = slice(P * h, P * (h + 1))
+                bank = psum.tile([P, BANK], F32, name="bank")
+                nc.tensor.matmul_mx(
+                    out=bank[:],
+                    lhsT=(xw[h][:, r] if r < PACK else next_w[:, cols]).bitcast(FP8X4),
+                    lhsT_scale=xs[h][:, r] if r < PACK else next_s[:, cols],
+                    rhs=ww[w][:].bitcast(FP4X4),
+                    rhs_scale=ws[w][:],
+                    start=True,
+                    stop=True,
+                )
+                banks[w, r] = bank[:].rearrange("p (m t) -> p t m", t=PACK)
             return banks
 
-        def copy_evens(t, banks):
-            for h in range(2):
-                for w in range(2):
-                    nc.scalar.copy(out=evens[:, t, w, HALF * h : HALF * (h + 1)], in_=banks[w, h][:, 0, :])
+        def keep_middle(banks):
+            mid = ring.tile([P, 2, PACK, P], F32, name="mid")
+            for w in range(2):
+                nc.scalar.copy(out=mid[:, w], in_=banks[w, 2])
+            return mid
 
-        def squares(banks):
-            sq = ring.tile([P, 2, 2, V], F32, name="sq")
-            for h in range(2):
-                for w in range(2):
-                    nc.scalar.activation(out=sq[:, w, :, HALF * h : HALF * (h + 1)], in_=banks[w, h], func=ACT.Square)
-            return sq
+        def terms(h, u, banks, mid):
+            sq = ring.tile([P, 2, 2, PACK, P], F32, name="sq")
+            nb = ring.tile([P, 2, PACK, P], F32, name="nb")
+            cx = ring.tile([P, 2, PACK, P], F32, name="cx")
+            for w in range(2):
+                nc.scalar.activation(out=sq[:, w, 0], in_=mid[:, w] if u else banks[w, 0], func=ACT.Square)
+                nc.scalar.activation(out=sq[:, w, 1], in_=banks[w, 2 * u + 1], func=ACT.Square)
+            for w in range(2):
+                nc.vector.tensor_tensor(nb[:, w], banks[w, 4 * u], mid[:, w], ALU.add)
+            for w in range(2):
+                nc.vector.tensor_tensor(cx[:, w], banks[w, 2 * u + 1], nb[:, w], ALU.mult)
+            if h == u:
+                return [sq[:, w, e] for w in range(2) for e in range(2)], cx
+            both = ring.tile([P, PACK, P], F32, name="both")
+            nc.gpsimd.tensor_tensor(both[:], sq[:, 0, 0], sq[:, 0, 1], ALU.add)
+            return [sq[:, 1, 0], sq[:, 1, 1], both[:]], cx
 
-        def add_parts(sq):
-            pw = ring.tile([P, 2, V], F32, name="pw")
-            nc.vector.tensor_tensor(pw[:], sq[:, 0], sq[:, 1], ALU.add)
-            return pw
+        def add_turned(region, parts):
+            for i, part in enumerate(parts):
+                nc.tensor.matmul(out=region, lhsT=part, rhs=ident[:], is_transpose=True, start=(i == 0), stop=(i == len(parts) - 1))
 
-        def add_pairs(t, pw):
-            nc.vector.tensor_tensor(power[t][:], pw[:, 0], pw[:, 1], ALU.add)
+        def sum_banks():
+            power = psum.tile([P, BANK], F32, name="power", tag="sums")
+            cross = psum.tile([P, BANK], F32, name="cross", tag="sums")
+            return power, cross
 
-        def neighbours(t):
-            nb = ring.tile([P, 2, V], F32, name="nb")
-            nc.vector.tensor_tensor(nb[:], evens[:, t, :, 0:V], evens[:, t, :, 1 : V + 1], ALU.add)
-            return nb
+        def sums(u, pairs, made):
+            sq, cx = made
+            for t in range(PACK):
+                cols = slice(HALF * (t % 2) + P * u, HALF * (t % 2) + P * (u + 1))
+                add_turned(pairs[t // 2][0][:, cols], [part[:, t] for part in sq])
+            for t in range(PACK):
+                cols = slice(HALF * (t % 2) + P * u, HALF * (t % 2) + P * (u + 1))
+                add_turned(pairs[t // 2][1][:, cols], [cx[:, w, t] for w in range(2)])
 
-        def cross(nb, banks):
-            cx = ring.tile([P, 2, V], F32, name="cx")
-            for h in range(2):
-                for w in range(2):
-                    cols = slice(HALF * h, HALF * (h + 1))
-                    nc.vector.tensor_tensor(cx[:, w, cols], banks[w, h][:, 1, :], nb[:, w, cols], ALU.mult)
-            return cx
+        def post(h, k, pair):
+            power, cross = (b[:].rearrange("p (j u q) -> p j q u", j=2, u=2) for b in pair)
+            cols = slice(HALF * h, HALF * (h + 1))
+            kept = corr[:, 2 * k : 2 * k + 2, cols].rearrange("p j (q u) -> p j q u", u=2)
+            if h == 0:
+                nc.scalar.copy(out=kept, in_=cross)
+            else:
+                nc.vector.tensor_copy(out=kept, in_=cross)
+            nc.scalar.activation(out=logd[k][:, :, cols].rearrange("p j (q u) -> p j q u", u=2), in_=power, func=ACT.Ln, bias=0.9)
+            for j in range(2):
+                t = 2 * k + j
+                nc.vector.scalar_tensor_tensor(
+                    noise[t][:, cols].rearrange("p (q u) -> p q u", u=2),
+                    power[:, j],
+                    0.4,
+                    corr[:, t, cols].rearrange("p (q u) -> p q u", u=2),
+                    ALU.add,
+                    ALU.subtract,
+                )
 
-        def add_cross(t, cx):
-            nc.vector.tensor_tensor(noise[t][:, V:], cx[:, 0], cx[:, 1], ALU.add)
+        pick_half(0)
+        banks = products(0, ((0, 2), (0, 0), (1, 2), (1, 0), (0, 1), (1, 1)))
+        mid = keep_middle(banks)
+        even = terms(0, 0, banks, mid)
+        pick_half(1)
+        shift()
+        banks = products(0, ((0, 4), (1, 4), (0, 3), (1, 3)))
+        odd = terms(0, 1, banks, mid)
+        pairs = [sum_banks(), sum_banks()]
+        banks = products(1, ((0, 2), (1, 2), (0, 0), (1, 0), (0, 1), (1, 1)))
+        sums(0, pairs, even)
+        mid = keep_middle(banks)
+        even = terms(1, 0, banks, mid)
+        banks = products(1, ((0, 4), (1, 4), (0, 3), (1, 3)))
+        sums(1, pairs, odd)
+        post(0, 0, pairs[0])
+        post(0, 1, pairs[1])
+        odd = terms(1, 1, banks, mid)
+        pairs = [sum_banks(), sum_banks()]
+        sums(0, pairs, even)
+        sums(1, pairs, odd)
+        post(1, 0, pairs[0])
+        post(1, 1, pairs[1])
 
-        def make_noise(t):
-            nc.vector.scalar_tensor_tensor(noise[t][:, :V], power[t][:], 0.4, noise[t][:, V:], ALU.add, ALU.subtract)
+        def gather_noise(t, h, on_scalar):
+            cols = slice(HALF * h, HALF * (h + 1))
+            window = noise[t][:].indirect(s1_t[:, 16 * h : 16 * (h + 1)])
+            if on_scalar:
+                nc.scalar.activation(out=noise_g[t][:, cols], in_=window, func=ACT.Copy)
+            else:
+                nc.vector.tensor_copy(noise_g[t][:, cols], window)
 
-        def log_power(t):
-            nc.scalar.activation(out=logd[t][:], in_=power[t][:], func=ACT.Ln, bias=0.9)
-
-        def gather_noise(t):
-            nc.scalar.activation(out=noise_g[t][:], in_=noise[t][:].indirect(s1_t[:]), func=ACT.Copy)
-
-        last = PACK - 1
-        for t in range(last):
-            banks = products(t)
-            copy_evens(t, banks)
-            sq = squares(banks)
-            nb = neighbours(t)
-            if t > 0:
-                make_noise(t - 1)
-                log_power(t - 1)
-            cx = cross(nb, banks)
-            pw = add_parts(sq)
-            add_cross(t, cx)
-            add_pairs(t, pw)
-            if t > 0:
-                gather_noise(t - 1)
-        banks = products(last)
-        sq = squares(banks)
-        log_power(last - 1)
-        copy_evens(last, banks)
-        pw = add_parts(sq)
-        make_noise(last - 1)
-        add_pairs(last, pw)
-        log_power(last)
-        gather_noise(last - 1)
-        nb = neighbours(last)
-        cx = cross(nb, banks)
-        add_cross(last, cx)
-        make_noise(last)
-
-        inv_last = keep.tile([P, V], F32, name="inv_last")
-        nc.scalar.activation(out=inv_last[:], in_=logd[last][:], func=ACT.Exp, scale=-1.0)
-        late = keep.tile([P, 2 * PACK - 1, V], F32, name="late", tag="hold")
+        inv_first = keep.tile([P, 2, V], F32, name="inv_first")
+        nc.scalar.activation(out=inv_first[:], in_=logd[1][:], func=ACT.Exp, scale=-1.0)
+        late = keep.tile([P, PACK + 2, V], F32, name="late", tag="hold")
         gain = [keep.tile([P, V], F32, name=f"gain{t}") for t in range(PACK)]
         hid = keep.tile([P, PACK, V], F32, name="hid")
 
-        def finish(h):
-            cols = slice(HALF * h, HALF * (h + 1))
-            hb = keep.tile([P, HALF, PACK], BF16, name=f"hb{h}", align_bytes=64)
-            nc.vector.tensor_copy(
+        def interleave(cols, engine):
+            width = cols.stop - cols.start
+            hb = keep.tile([P, width, PACK], BF16, name=f"hb{cols.start}", align_bytes=64)
+            engine(
                 out=hb[:].rearrange("p (c i) t -> p c t i", i=4),
                 in_=hid[:, :, cols].rearrange("p t (c i) -> p c t i", i=4),
             )
             return hb
 
-        def last_product(h, hb):
-            cols = slice(HALF * h, HALF * (h + 1))
-            codes = keep.tile([P, HALF], U32, name=f"codes{h}", align_bytes=64)
-            scales = keep.tile([P, HALF], U8, name=f"scales{h}", align_bytes=64)
+        def last_product(cols, hb, queue):
+            width = cols.stop - cols.start
+            codes = keep.tile([P, width], U32, name=f"codes{cols.start}", align_bytes=64)
+            scales = keep.tile([P, width], U8, name=f"scales{cols.start}", align_bytes=64)
             nc.vector.quantize_mx(out=codes[:].bitcast(FP8X4), scales=scales[:], in_=hb[:].rearrange("p c t -> p (c t)"))
             bank = psum.tile([P, BANK], F32, name="bank")
             for m in range(2):
                 nc.tensor.matmul_mx(
-                    out=bank[:, HALF * m : HALF * (m + 1)],
+                    out=bank[:, width * m : width * (m + 1)],
                     lhsT=w3w[:, 2 * P * m : 2 * P * (m + 1)].bitcast(FP4X4),
                     lhsT_scale=w3s[:, P * m : P * (m + 1)],
                     rhs=codes[:].bitcast(FP8X4),
@@ -224,13 +240,13 @@ def tile_picked_ybeamfr_mul_p_kernel(
                     start=True,
                     stop=True,
                 )
-            res = keep.tile([P, 2, HALF], F32, name=f"res{h}")
-            nc.scalar.copy(out=res[:].rearrange("p m v -> p (m v)"), in_=bank[:])
-            nc.sync.dma_start(out=out[:, cols].rearrange("(m p) v -> p m v", p=P), in_=res[:])
+            res = keep.tile([P, 2, width], F32, name=f"res{cols.start}")
+            nc.scalar.copy(out=res[:].rearrange("p m v -> p (m v)"), in_=bank[:, : 2 * width])
+            queue.dma_start(out=out[:, cols].rearrange("(m p) v -> p m v", p=P), in_=res[:])
 
-        def gather_gain(t, h):
-            cols = slice(HALF * h, HALF * (h + 1))
-            nc.vector.tensor_tensor(hid[:, t, cols], gain[t][:].indirect(s2_t[:, 16 * h : 16 * (h + 1)]), noise_g[t][:, cols], ALU.mult)
+        def gather_gain(t, cols):
+            entries = s2_t[:, cols.start // 16 : cols.stop // 16]
+            nc.vector.tensor_tensor(hid[:, t, cols], gain[t][:].indirect(entries), noise_g[t][:, cols], ALU.mult)
 
         def gather_gain_scalar(t):
             picked = ring.tile([P, V], F32, name="picked")
@@ -240,28 +256,36 @@ def tile_picked_ybeamfr_mul_p_kernel(
             return picked
 
         def make_gain(t):
-            if t < last:
-                inv = late[:, PACK + t]
-                nc.scalar.activation(out=inv, in_=logd[t][:], func=ACT.Exp, scale=-1.0)
-            else:
-                inv = inv_last[:]
-            nc.scalar.activation(out=late[:, t], in_=noise[t][:, V:], func=ACT.Tanh)
+            inv = inv_first[:, t - 2] if t >= 2 else late[:, PACK + t]
+            nc.scalar.activation(out=late[:, t], in_=corr[:, t], func=ACT.Tanh)
             nc.vector.scalar_tensor_tensor(gain[t][:], late[:, t], unit_t[:, t : t + 1], inv, ALU.mult, ALU.mult)
 
-        make_gain(0)
-        make_gain(1)
-        gather_gain(0, 0)
-        gather_gain(0, 1)
+        for t in (2, 3):
+            for h in range(2):
+                gather_noise(t, h, False)
         make_gain(2)
         make_gain(3)
-        gather_noise(3)
-        picked = gather_gain_scalar(2)
-        gather_gain(1, 0)
-        gather_gain(1, 1)
-        gather_gain(3, 0)
-        nc.vector.tensor_tensor(hid[:, 2], picked[:], noise_g[2][:], ALU.mult)
-        hb0 = finish(0)
-        gather_gain(last, 1)
-        last_product(0, hb0)
-        hb1 = finish(1)
-        last_product(1, hb1)
+        nc.scalar.activation(out=late[:, PACK:], in_=logd[0][:], func=ACT.Exp, scale=-1.0)
+        halves = (slice(0, HALF), slice(HALF, V))
+        pieces = (slice(0, HALF), slice(HALF, HALF + P), slice(HALF + P, V))
+        for cols in halves:
+            gather_gain(2, cols)
+        make_gain(0)
+        make_gain(1)
+        gather_noise(0, 0, True)
+        gather_noise(0, 1, True)
+        for cols in halves:
+            gather_gain(3, cols)
+        gather_noise(1, 0, True)
+        picked = gather_gain_scalar(0)
+        gather_noise(1, 1, True)
+        gather_gain(1, pieces[0])
+        nc.vector.tensor_tensor(hid[:, 0], picked[:], noise_g[0][:], ALU.mult)
+        gather_gain(1, pieces[1])
+        hb0 = interleave(pieces[0], nc.scalar.copy)
+        gather_gain(1, pieces[2])
+        hb1 = interleave(pieces[1], nc.vector.tensor_copy)
+        hb2 = interleave(pieces[2], nc.vector.tensor_copy)
+        last_product(pieces[1], hb1, nc.sync)
+        last_product(pieces[0], hb0, nc.sync)
+        last_product(pieces[2], hb2, nc.scalar)

@@ -30,7 +30,8 @@ def tile_picked_ybeamfr_mul_p_kernel(
     with ExitStack() as ctx:
         keep = ctx.enter_context(tc.tile_pool(name="keep", bufs=1))
         ring = ctx.enter_context(tc.tile_pool(name="ring", bufs=2))
-        quad = ctx.enter_context(tc.tile_pool(name="quad", bufs=4))
+        squares = ctx.enter_context(tc.tile_pool(name="squares", bufs=8))
+        picks = ctx.enter_context(tc.tile_pool(name="picks", bufs=1))
         psum = ctx.enter_context(tc.psum_pool(name="psum", bufs=4))
 
         offs_t = keep.tile([P, S // 16], U16, name="offs_t")
@@ -77,8 +78,8 @@ def tile_picked_ybeamfr_mul_p_kernel(
         xw = [keep.tile([P, PACK, P], U32, name=f"xw{h}", align_bytes=64) for h in range(2)]
         xs = [keep.tile([P, PACK, P], U8, name=f"xs{h}", align_bytes=64) for h in range(2)]
 
-        def pick(h, window, dealt, dtype, line, name, tag):
-            picked_x = keep.tile([P, BANK], dtype, name=name, tag=tag, align_bytes=64)
+        def pick(h, window, dealt, dtype, line, name, offset):
+            picked_x = picks.tile([P, BANK], dtype, name=name, offset=offset, align_bytes=64)
             nc.vector.tensor_copy(picked_x[:], window.indirect(offs_t[:, 32 * h : 32 * (h + 1)]))
             nc.vector.tensor_copy(
                 out=dealt[:].rearrange("p r (c i) -> p c r i", i=line),
@@ -86,8 +87,8 @@ def tile_picked_ybeamfr_mul_p_kernel(
             )
 
         def pick_half(h):
-            pick(h, xs_raw[:], xs[h], U8, 16, f"ps{h}", "picked" if h else "picked_first")
-            pick(h, xw_raw[:].bitcast(U32), xw[h], U32, 4, f"pw{h}", "picked")
+            pick(h, xs_raw[:], xs[h], U8, 16, f"ps{h}", 0 if h else 3072)
+            pick(h, xw_raw[:].bitcast(U32), xw[h], U32, 4, f"pw{h}", 1024 * h)
 
         def shift():
             for shifted, dealt in ((next_w, xw), (next_s, xs)):
@@ -99,11 +100,11 @@ def tile_picked_ybeamfr_mul_p_kernel(
         logd = [keep.tile([P, 2, V], F32, name="logd0"), keep.tile([P, 2, V], F32, name="logd1", tag="hold")]
         noise_g = [keep.tile([P, V], F32, name=f"noise_g{t}") for t in range(PACK)]
 
-        def products(h, order):
+        def products(h, order, tag="bank"):
             banks = {}
             for w, r in order:
                 cols = slice(P * h, P * (h + 1))
-                bank = psum.tile([P, BANK], F32, name="bank")
+                bank = psum.tile([P, BANK], F32, name="bank", tag=tag)
                 nc.tensor.matmul_mx(
                     out=bank[:],
                     lhsT=(xw[h][:, r] if r < PACK else next_w[:, cols]).bitcast(FP8X4),
@@ -116,90 +117,114 @@ def tile_picked_ybeamfr_mul_p_kernel(
                 banks[w, r] = bank[:].rearrange("p (m t) -> p t m", t=PACK)
             return banks
 
-        def keep_middle(banks):
+        def keep_middle(h):
+            banks = products(h, ((0, 2), (1, 2)), "sums")
             mid = ring.tile([P, 2, PACK, P], F32, name="mid")
             for w in range(2):
                 nc.scalar.copy(out=mid[:, w], in_=banks[w, 2])
             return mid
 
-        def terms(h, u, banks, mid):
-            sq = ring.tile([P, 2, 2, PACK, P], F32, name="sq")
+        def square(src):
+            sq = squares.tile([P, PACK, P], F32, name="sq")
+            nc.scalar.activation(out=sq[:], in_=src, func=ACT.Square)
+            return sq[:]
+
+        def pre_add(a, b, first=False):
+            if first:
+                both = picks.tile([P, PACK, P], F32, name="both_first", offset=1024, align_bytes=64)
+            else:
+                both = squares.tile([P, PACK, P], F32, name="both")
+            nc.gpsimd.tensor_tensor(both[:], a, b, ALU.add)
+            return both[:]
+
+        def cross_terms(u, banks, mid):
             nb = ring.tile([P, 2, PACK, P], F32, name="nb")
             cx = ring.tile([P, 2, PACK, P], F32, name="cx")
-            for w in range(2):
-                nc.scalar.activation(out=sq[:, w, 0], in_=mid[:, w] if u else banks[w, 0], func=ACT.Square)
-                nc.scalar.activation(out=sq[:, w, 1], in_=banks[w, 2 * u + 1], func=ACT.Square)
             for w in range(2):
                 nc.vector.tensor_tensor(nb[:, w], banks[w, 4 * u], mid[:, w], ALU.add)
             for w in range(2):
                 nc.vector.tensor_tensor(cx[:, w], banks[w, 2 * u + 1], nb[:, w], ALU.mult)
-            if h == u:
-                return [sq[:, w, e] for w in range(2) for e in range(2)], cx
-            both = ring.tile([P, PACK, P], F32, name="both")
-            nc.gpsimd.tensor_tensor(both[:], sq[:, 0, 0], sq[:, 0, 1], ALU.add)
-            return [sq[:, 1, 0], sq[:, 1, 1], both[:]], cx
+            return [cx[:, 0], cx[:, 1]]
 
         def add_turned(region, parts):
             for i, part in enumerate(parts):
                 nc.tensor.matmul(out=region, lhsT=part, rhs=ident[:], is_transpose=True, start=(i == 0), stop=(i == len(parts) - 1))
 
-        def sum_banks():
-            power = psum.tile([P, BANK], F32, name="power", tag="sums")
-            cross = psum.tile([P, BANK], F32, name="cross", tag="sums")
-            return power, cross
+        def sum_banks(tag):
+            return [psum.tile([P, BANK], F32, name="sums", tag=tag) for k in range(2)]
 
-        def sums(u, pairs, made):
-            sq, cx = made
+        def sums(u, banks, parts):
             for t in range(PACK):
                 cols = slice(HALF * (t % 2) + P * u, HALF * (t % 2) + P * (u + 1))
-                add_turned(pairs[t // 2][0][:, cols], [part[:, t] for part in sq])
-            for t in range(PACK):
-                cols = slice(HALF * (t % 2) + P * u, HALF * (t % 2) + P * (u + 1))
-                add_turned(pairs[t // 2][1][:, cols], [cx[:, w, t] for w in range(2)])
+                add_turned(banks[t // 2][:, cols], [part[:, t] for part in parts])
 
-        def post(h, k, pair):
-            power, cross = (b[:].rearrange("p (j u q) -> p j q u", j=2, u=2) for b in pair)
+        def by_pair(ap):
+            return ap.rearrange("p j (q u) -> p j q u", u=2)
+
+        def as_pairs(bank):
+            return bank[:].rearrange("p (j u q) -> p j q u", j=2, u=2)
+
+        def keep_cross(h, k, cross, engine):
+            engine(out=by_pair(corr[:, 2 * k : 2 * k + 2, HALF * h : HALF * (h + 1)]), in_=as_pairs(cross[k]))
+
+        def log_power(h, k, power):
+            nc.scalar.activation(out=by_pair(logd[k][:, :, HALF * h : HALF * (h + 1)]), in_=as_pairs(power[k]), func=ACT.Ln, bias=0.9)
+
+        def make_noise(h, t, power):
             cols = slice(HALF * h, HALF * (h + 1))
-            kept = corr[:, 2 * k : 2 * k + 2, cols].rearrange("p j (q u) -> p j q u", u=2)
-            if h == 0:
-                nc.scalar.copy(out=kept, in_=cross)
-            else:
-                nc.vector.tensor_copy(out=kept, in_=cross)
-            nc.scalar.activation(out=logd[k][:, :, cols].rearrange("p j (q u) -> p j q u", u=2), in_=power, func=ACT.Ln, bias=0.9)
-            for j in range(2):
-                t = 2 * k + j
-                nc.vector.scalar_tensor_tensor(
-                    noise[t][:, cols].rearrange("p (q u) -> p q u", u=2),
-                    power[:, j],
-                    0.4,
-                    corr[:, t, cols].rearrange("p (q u) -> p q u", u=2),
-                    ALU.add,
-                    ALU.subtract,
-                )
+            nc.vector.scalar_tensor_tensor(
+                noise[t][:, cols].rearrange("p (q u) -> p q u", u=2),
+                as_pairs(power[t // 2])[:, t % 2],
+                0.4,
+                corr[:, t, cols].rearrange("p (q u) -> p q u", u=2),
+                ALU.add,
+                ALU.subtract,
+            )
 
+        first_pair, second_pair = ((0, 0), (1, 0), (0, 1), (1, 1)), ((0, 4), (1, 4), (0, 3), (1, 3))
         pick_half(0)
-        banks = products(0, ((0, 2), (0, 0), (1, 2), (1, 0), (0, 1), (1, 1)))
-        mid = keep_middle(banks)
-        even = terms(0, 0, banks, mid)
         pick_half(1)
         shift()
-        banks = products(0, ((0, 4), (1, 4), (0, 3), (1, 3)))
-        odd = terms(0, 1, banks, mid)
-        pairs = [sum_banks(), sum_banks()]
-        banks = products(1, ((0, 2), (1, 2), (0, 0), (1, 0), (0, 1), (1, 1)))
-        sums(0, pairs, even)
-        mid = keep_middle(banks)
-        even = terms(1, 0, banks, mid)
-        banks = products(1, ((0, 4), (1, 4), (0, 3), (1, 3)))
-        sums(1, pairs, odd)
-        post(0, 0, pairs[0])
-        post(0, 1, pairs[1])
-        odd = terms(1, 1, banks, mid)
-        pairs = [sum_banks(), sum_banks()]
-        sums(0, pairs, even)
-        sums(1, pairs, odd)
-        post(1, 0, pairs[0])
-        post(1, 1, pairs[1])
+        mid0 = keep_middle(0)
+        banks = products(0, first_pair)
+        sq = [square(banks[key]) for key in first_pair]
+        even_power = [pre_add(sq[0], sq[1], True), pre_add(sq[2], sq[3])]
+        even_cross = cross_terms(0, banks, mid0)
+        middles = pre_add(square(mid0[:, 0]), square(mid0[:, 1]))
+        banks = products(0, second_pair)
+        mid1 = keep_middle(1)
+        odd_power = [middles, square(banks[0, 3]), square(banks[1, 3])]
+        odd_cross = cross_terms(1, banks, mid0)
+        middles = pre_add(square(mid1[:, 0]), square(mid1[:, 1]))
+        cross, power = sum_banks("sums"), sum_banks("sums")
+        banks = products(1, first_pair)
+        sums(0, cross, even_cross)
+        sums(0, power, even_power)
+        sq = [square(banks[key]) for key in first_pair]
+        even_power = [pre_add(sq[0], sq[1]), sq[2], sq[3]]
+        even_cross = cross_terms(0, banks, mid1)
+        banks = products(1, second_pair)
+        sums(1, cross, odd_cross)
+        sums(1, power, odd_power)
+        for k in range(2):
+            keep_cross(0, k, cross, nc.scalar.copy)
+        for t in range(PACK):
+            make_noise(0, t, power)
+        odd_power = [middles, square(banks[0, 3]), square(banks[1, 3])]
+        odd_cross = cross_terms(1, banks, mid1)
+        for k in range(2):
+            log_power(0, k, power)
+        power, cross = sum_banks("sums"), sum_banks("bank")
+        sums(0, power, even_power)
+        sums(0, cross, even_cross)
+        sums(1, power, odd_power)
+        sums(1, cross, odd_cross)
+        for k in range(2):
+            log_power(1, k, power)
+        for k in (1, 0):
+            keep_cross(1, k, cross, nc.vector.tensor_copy)
+            make_noise(1, 2 * k, power)
+            make_noise(1, 2 * k + 1, power)
 
         def gather_noise(t, h, on_scalar):
             cols = slice(HALF * h, HALF * (h + 1))
@@ -224,7 +249,7 @@ def tile_picked_ybeamfr_mul_p_kernel(
             )
             return hb
 
-        def last_product(cols, hb, queue):
+        def last_product(cols, hb, engine, queue):
             width = cols.stop - cols.start
             codes = keep.tile([P, width], U32, name=f"codes{cols.start}", align_bytes=64)
             scales = keep.tile([P, width], U8, name=f"scales{cols.start}", align_bytes=64)
@@ -241,7 +266,7 @@ def tile_picked_ybeamfr_mul_p_kernel(
                     stop=True,
                 )
             res = keep.tile([P, 2, width], F32, name=f"res{cols.start}")
-            nc.scalar.copy(out=res[:].rearrange("p m v -> p (m v)"), in_=bank[:, : 2 * width])
+            engine(out=res[:].rearrange("p m v -> p (m v)"), in_=bank[:, : 2 * width])
             queue.dma_start(out=out[:, cols].rearrange("(m p) v -> p m v", p=P), in_=res[:])
 
         def gather_gain(t, cols):
@@ -286,6 +311,6 @@ def tile_picked_ybeamfr_mul_p_kernel(
         gather_gain(1, pieces[2])
         hb1 = interleave(pieces[1], nc.vector.tensor_copy)
         hb2 = interleave(pieces[2], nc.vector.tensor_copy)
-        last_product(pieces[1], hb1, nc.sync)
-        last_product(pieces[0], hb0, nc.sync)
-        last_product(pieces[2], hb2, nc.scalar)
+        last_product(pieces[1], hb1, nc.scalar.copy, nc.sync)
+        last_product(pieces[0], hb0, nc.scalar.copy, nc.scalar)
+        last_product(pieces[2], hb2, nc.vector.tensor_copy, nc.sync)

from contextlib import ExitStack

import concourse.mybir as mybir
from concourse.masks import make_identity

K, T, S, H, V, N = 512, 2048, 1024, 512, 512, 256
FLOPS = 2 * K * H * S * 2 + 2 * H * N * V

F32 = mybir.dt.float32
BF16 = mybir.dt.bfloat16
I32 = mybir.dt.int32
U32 = mybir.dt.uint32
U16 = mybir.dt.uint16
U8 = mybir.dt.uint8
FP8X4 = mybir.dt.float8_e4m3fn_x4
FP4X4 = mybir.dt.float4_e2m1fn_x4
ACT = mybir.ActivationFunctionType
ALU = mybir.AluOpType

P = 128
PACK = 4
BANK = 512
HALF = 256


def tile_picked_ybeamfr_mul_p_kernel(
    tc, x_words, x_scales, w1_words, w1_scales, w2_words, w2_scales, unit, w3_words, w3_scales, offs, s1, s2, out
):
    nc = tc.nc
    with ExitStack() as ctx:
        keep = ctx.enter_context(tc.tile_pool(name="keep", bufs=1))
        ring = ctx.enter_context(tc.tile_pool(name="ring", bufs=2))
        squares = ctx.enter_context(tc.tile_pool(name="squares", bufs=8))
        picks = ctx.enter_context(tc.tile_pool(name="picks", bufs=1))
        psum = ctx.enter_context(tc.psum_pool(name="psum", bufs=4))

        offs_t = keep.tile([P, S // 16], U16, name="offs_t")
        s1_t = keep.tile([P, V // 16], U16, name="s1_t")
        s2_t = keep.tile([P, V // 16], U16, name="s2_t")
        xw_raw = keep.tile([P, T], I32, name="xw_raw", align_bytes=64)
        xs_raw = keep.tile([P, T], U8, name="xs_raw", align_bytes=64)
        ww = [keep.tile([P, 2 * H], U8, name=f"ww{w}", align_bytes=64) for w in range(2)]
        ws = [keep.tile([P, H], U8, name=f"ws{w}", align_bytes=64) for w in range(2)]
        w3w = keep.tile([P, 2 * N], U8, name="w3w", align_bytes=64)
        w3s = keep.tile([P, N], U8, name="w3s", align_bytes=64)
        unit_t = keep.tile([P, PACK], F32, name="unit_t")
        ident = keep.tile([P, P], F32, name="ident")
        next_w = keep.tile([P, HALF], U32, name="next_w", align_bytes=64)
        next_s = keep.tile([P, HALF], U8, name="next_s", align_bytes=64)

        nc.gpsimd.memset(xs_raw[:].bitcast(I32), 0)
        nc.gpsimd.memset(ws[1][:].bitcast(I32), 0)
        nc.gpsimd.memset(ws[0][:].bitcast(I32), 0)

        def load_scales(queue, plane, rows, q):
            queue.dma_start(out=plane[32 * q : 32 * q + 4].bitcast(I32), in_=rows[0, 4 * q : 4 * q + 4, :].bitcast(I32))

        nc.sync.dma_start(offs_t[:], offs)
        nc.sync.dma_start(out=xw_raw[:], in_=x_words[0].rearrange("p c r -> p (c r)").bitcast(I32))
        for q in range(4):
            load_scales(nc.scalar, xs_raw[:], x_scales, q)
        nc.gpsimd.dma_start(out=ww[0][:].bitcast(I32), in_=w1_words[0].bitcast(I32))
        nc.gpsimd.dma_start(out=ww[1][:].bitcast(I32), in_=w2_words[0].bitcast(I32))
        for q in range(4):
            load_scales(nc.scalar, ws[1][:], w2_scales, q)
            load_scales(nc.sync, ws[0][:], w1_scales, q)
        nc.vector.memset(next_w[:, HALF - 8 :].bitcast(I32), 0)
        nc.vector.memset(next_s[:, HALF - 32 :].bitcast(I32), 0)
        make_identity(nc, ident[:])
        nc.gpsimd.memset(w3s[:].bitcast(I32), 0)
        nc.sync.dma_start(s1_t[:], s1)
        nc.sync.dma_start(s2_t[:], s2)
        nc.gpsimd.dma_start(out=unit_t[:], in_=unit.rearrange("(p t) o -> p (t o)", t=PACK))
        nc.gpsimd.dma_start(out=w3w[:].bitcast(I32), in_=w3_words[0].bitcast(I32))
        for q in range(4):
            load_scales(nc.sync, w3s[:], w3_scales, q)

        xw = [keep.tile([P, PACK, P], U32, name=f"xw{h}", align_bytes=64) for h in range(2)]
        xs = [keep.tile([P, PACK, P], U8, name=f"xs{h}", align_bytes=64) for h in range(2)]

        def pick(h, window, dealt, dtype, line, name, offset):
            picked_x = picks.tile([P, BANK], dtype, name=name, offset=offset, align_bytes=64)
            nc.vector.tensor_copy(picked_x[:], window.indirect(offs_t[:, 32 * h : 32 * (h + 1)]))
            nc.vector.tensor_copy(
                out=dealt[:].rearrange("p r (c i) -> p c r i", i=line),
                in_=picked_x[:].rearrange("p (c i r) -> p c r i", i=line, r=PACK),
            )

        def pick_half(h):
            pick(h, xs_raw[:], xs[h], U8, 16, f"ps{h}", 0 if h else 3072)
            pick(h, xw_raw[:].bitcast(U32), xw[h], U32, 4, f"pw{h}", 1024 * h)

        def shift():
            for shifted, dealt in ((next_w, xw), (next_s, xs)):
                nc.vector.tensor_copy(out=shifted[:, 0 : P - 1], in_=dealt[0][:, 0, 1:])
                nc.vector.tensor_copy(out=shifted[:, P - 1 : 2 * P - 1], in_=dealt[1][:, 0, :])

        noise = [keep.tile([P, V], F32, name=f"noise{t}") for t in range(PACK)]
        corr = keep.tile([P, PACK, V], F32, name="corr")
        logd = [keep.tile([P, 2, V], F32, name="logd0"), keep.tile([P, 2, V], F32, name="logd1", tag="hold")]
        noise_g = [keep.tile([P, V], F32, name=f"noise_g{t}") for t in range(PACK)]

        def products(h, order, tag="bank"):
            banks = {}
            for w, r in order:
                cols = slice(P * h, P * (h + 1))
                bank = psum.tile([P, BANK], F32, name="bank", tag=tag)
                nc.tensor.matmul_mx(
                    out=bank[:],
                    lhsT=(xw[h][:, r] if r < PACK else next_w[:, cols]).bitcast(FP8X4),
                    lhsT_scale=xs[h][:, r] if r < PACK else next_s[:, cols],
                    rhs=ww[w][:].bitcast(FP4X4),
                    rhs_scale=ws[w][:],
                    start=True,
                    stop=True,
                )
                banks[w, r] = bank[:].rearrange("p (m t) -> p t m", t=PACK)
            return banks

        def keep_middle(h):
            banks = products(h, ((0, 2), (1, 2)), "sums")
            mid = ring.tile([P, 2, PACK, P], F32, name="mid")
            for w in range(2):
                nc.scalar.copy(out=mid[:, w], in_=banks[w, 2])
            return mid

        def square(src):
            sq = squares.tile([P, PACK, P], F32, name="sq")
            nc.scalar.activation(out=sq[:], in_=src, func=ACT.Square)
            return sq[:]

        def pre_add(a, b, first=False):
            if first:
                both = picks.tile([P, PACK, P], F32, name="both_first", offset=1024, align_bytes=64)
            else:
                both = squares.tile([P, PACK, P], F32, name="both")
            nc.gpsimd.tensor_tensor(both[:], a, b, ALU.add)
            return both[:]

        def cross_terms(u, banks, mid):
            nb = ring.tile([P, 2, PACK, P], F32, name="nb")
            cx = ring.tile([P, 2, PACK, P], F32, name="cx")
            for w in range(2):
                nc.vector.tensor_tensor(nb[:, w], banks[w, 4 * u], mid[:, w], ALU.add)
            for w in range(2):
                nc.vector.tensor_tensor(cx[:, w], banks[w, 2 * u + 1], nb[:, w], ALU.mult)
            return [cx[:, 0], cx[:, 1]]

        def add_turned(region, parts):
            for i, part in enumerate(parts):
                nc.tensor.matmul(out=region, lhsT=part, rhs=ident[:], is_transpose=True, start=(i == 0), stop=(i == len(parts) - 1))

        def sum_banks(tag):
            return [psum.tile([P, BANK], F32, name="sums", tag=tag) for k in range(2)]

        def sums(u, banks, parts):
            for t in range(PACK):
                cols = slice(HALF * (t % 2) + P * u, HALF * (t % 2) + P * (u + 1))
                add_turned(banks[t // 2][:, cols], [part[:, t] for part in parts])

        def by_pair(ap):
            return ap.rearrange("p j (q u) -> p j q u", u=2)

        def as_pairs(bank):
            return bank[:].rearrange("p (j u q) -> p j q u", j=2, u=2)

        def keep_cross(h, k, cross, engine):
            engine(out=by_pair(corr[:, 2 * k : 2 * k + 2, HALF * h : HALF * (h + 1)]), in_=as_pairs(cross[k]))

        def log_power(h, k, power):
            nc.scalar.activation(out=by_pair(logd[k][:, :, HALF * h : HALF * (h + 1)]), in_=as_pairs(power[k]), func=ACT.Ln, bias=0.9)

        def make_noise(h, t, power):
            cols = slice(HALF * h, HALF * (h + 1))
            nc.vector.scalar_tensor_tensor(
                noise[t][:, cols].rearrange("p (q u) -> p q u", u=2),
                as_pairs(power[t // 2])[:, t % 2],
                0.4,
                corr[:, t, cols].rearrange("p (q u) -> p q u", u=2),
                ALU.add,
                ALU.subtract,
            )

        first_pair, second_pair = ((0, 0), (1, 0), (0, 1), (1, 1)), ((0, 4), (1, 4), (0, 3), (1, 3))
        pick_half(0)
        pick_half(1)
        shift()
        mid0 = keep_middle(0)
        banks = products(0, first_pair)
        sq = [square(banks[key]) for key in first_pair]
        even_power = [pre_add(sq[0], sq[1], True), pre_add(sq[2], sq[3])]
        even_cross = cross_terms(0, banks, mid0)
        middles = pre_add(square(mid0[:, 0]), square(mid0[:, 1]))
        banks = products(0, second_pair)
        mid1 = keep_middle(1)
        odd_power = [middles, square(banks[0, 3]), square(banks[1, 3])]
        odd_cross = cross_terms(1, banks, mid0)
        middles = pre_add(square(mid1[:, 0]), square(mid1[:, 1]))
        cross, power = sum_banks("sums"), sum_banks("sums")
        banks = products(1, first_pair)
        sums(0, cross, even_cross)
        sums(0, power, even_power)
        sq = [square(banks[key]) for key in first_pair]
        even_power = [pre_add(sq[0], sq[1]), sq[2], sq[3]]
        even_cross = cross_terms(0, banks, mid1)
        banks = products(1, second_pair)
        sums(1, cross, odd_cross)
        sums(1, power, odd_power)
        for k in range(2):
            keep_cross(0, k, cross, nc.scalar.copy)
        for t in range(PACK):
            make_noise(0, t, power)
        odd_power = [middles, square(banks[0, 3]), square(banks[1, 3])]
        odd_cross = cross_terms(1, banks, mid1)
        for k in range(2):
            log_power(0, k, power)
        power, cross = sum_banks("sums"), sum_banks("bank")
        sums(0, power, even_power)
        sums(0, cross, even_cross)
        sums(1, power, odd_power)
        sums(1, cross, odd_cross)
        for k in range(2):
            log_power(1, k, power)
        for k in (1, 0):
            keep_cross(1, k, cross, nc.vector.tensor_copy)
            make_noise(1, 2 * k, power)
            make_noise(1, 2 * k + 1, power)

        def gather_noise(t, h, on_scalar):
            cols = slice(HALF * h, HALF * (h + 1))
            window = noise[t][:].indirect(s1_t[:, 16 * h : 16 * (h + 1)])
            if on_scalar:
                nc.scalar.activation(out=noise_g[t][:, cols], in_=window, func=ACT.Copy)
            else:
                nc.vector.tensor_copy(noise_g[t][:, cols], window)

        inv_first = keep.tile([P, 2, V], F32, name="inv_first")
        nc.scalar.activation(out=inv_first[:], in_=logd[1][:], func=ACT.Exp, scale=-1.0)
        late = keep.tile([P, PACK + 2, V], F32, name="late", tag="hold")
        gain = [keep.tile([P, V], F32, name=f"gain{t}") for t in range(PACK)]
        hid = keep.tile([P, PACK, V], F32, name="hid")

        def interleave(cols, engine):
            width = cols.stop - cols.start
            hb = keep.tile([P, width, PACK], BF16, name=f"hb{cols.start}", align_bytes=64)
            engine(
                out=hb[:].rearrange("p (c i) t -> p c t i", i=4),
                in_=hid[:, :, cols].rearrange("p t (c i) -> p c t i", i=4),
            )
            return hb

        def last_product(cols, hb, engine, queue):
            width = cols.stop - cols.start
            codes = keep.tile([P, width], U32, name=f"codes{cols.start}", align_bytes=64)
            scales = keep.tile([P, width], U8, name=f"scales{cols.start}", align_bytes=64)
            nc.vector.quantize_mx(out=codes[:].bitcast(FP8X4), scales=scales[:], in_=hb[:].rearrange("p c t -> p (c t)"))
            bank = psum.tile([P, BANK], F32, name="bank")
            for m in range(2):
                nc.tensor.matmul_mx(
                    out=bank[:, width * m : width * (m + 1)],
                    lhsT=w3w[:, 2 * P * m : 2 * P * (m + 1)].bitcast(FP4X4),
                    lhsT_scale=w3s[:, P * m : P * (m + 1)],
                    rhs=codes[:].bitcast(FP8X4),
                    rhs_scale=scales[:],
                    start=True,
                    stop=True,
                )
            res = keep.tile([P, 2, width], F32, name=f"res{cols.start}")
            engine(out=res[:].rearrange("p m v -> p (m v)"), in_=bank[:, : 2 * width])
            queue.dma_start(out=out[:, cols].rearrange("(m p) v -> p m v", p=P), in_=res[:])

        def gather_gain(t, cols):
            entries = s2_t[:, cols.start // 16 : cols.stop // 16]
            nc.vector.tensor_tensor(hid[:, t, cols], gain[t][:].indirect(entries), noise_g[t][:, cols], ALU.mult)

        def gather_gain_scalar(t):
            picked = ring.tile([P, V], F32, name="picked")
            for h in range(2):
                cols = slice(HALF * h, HALF * (h + 1))
                nc.scalar.activation(out=picked[:, cols], in_=gain[t][:].indirect(s2_t[:, 16 * h : 16 * (h + 1)]), func=ACT.Copy)
            return picked

        def make_gain(t):
            inv = inv_first[:, t - 2] if t >= 2 else late[:, PACK + t]
            nc.scalar.activation(out=late[:, t], in_=corr[:, t], func=ACT.Tanh)
            nc.vector.scalar_tensor_tensor(gain[t][:], late[:, t], unit_t[:, t : t + 1], inv, ALU.mult, ALU.mult)

        for t in (2, 3):
            for h in range(2):
                gather_noise(t, h, False)
        make_gain(2)
        make_gain(3)
        nc.scalar.activation(out=late[:, PACK:], in_=logd[0][:], func=ACT.Exp, scale=-1.0)
        halves = (slice(0, HALF), slice(HALF, V))
        pieces = (slice(0, HALF), slice(HALF, HALF + P), slice(HALF + P, V))
        for cols in halves:
            gather_gain(2, cols)
        make_gain(0)
        make_gain(1)
        gather_noise(0, 0, True)
        gather_noise(0, 1, True)
        for cols in halves:
            gather_gain(3, cols)
        gather_noise(1, 0, True)
        picked = gather_gain_scalar(0)
        gather_noise(1, 1, True)
        gather_gain(1, pieces[0])
        nc.vector.tensor_tensor(hid[:, 0], picked[:], noise_g[0][:], ALU.mult)
        gather_gain(1, pieces[1])
        hb0 = interleave(pieces[0], nc.scalar.copy)
        gather_gain(1, pieces[2])
        hb1 = interleave(pieces[1], nc.vector.tensor_copy)
        hb2 = interleave(pieces[2], nc.vector.tensor_copy)
        last_product(pieces[1], hb1, nc.scalar.copy, nc.sync)
        last_product(pieces[0], hb0, nc.scalar.copy, nc.scalar)
        last_product(pieces[2], hb2, nc.vector.tensor_copy, nc.sync)
